import numpy as np
import ml_dtypes


def mxq(x, axis, fmt="e4m3"):
    dtype, down = {"e4m3": (ml_dtypes.float8_e4m3fn, 7), "e5m2": (ml_dtypes.float8_e5m2, 14)}[fmt]
    v = np.moveaxis(np.asarray(x, np.float32).astype(ml_dtypes.bfloat16).astype(np.float64), axis, -1)
    blocks = v.reshape(v.shape[:-1] + (-1, 32))
    amax = np.abs(blocks).max(-1, keepdims=True)
    byte = np.maximum(np.where(amax > 0, np.frexp(amax)[1] - 1 + 127, 0) - down, 1)
    scale = np.exp2(byte - 127.0)
    codes = (blocks / scale).astype(np.float32).astype(dtype).astype(np.float64)
    return np.moveaxis((codes * scale).reshape(v.shape), -1, axis)


WIDE = False


def mx_kscale(k):
    if not WIDE:
        return np.ones(k)
    levels = np.array([10, -10, 5, -5, 0])
    if k % 512:
        return np.exp2(np.random.permutation(np.resize(levels, k // 32))).repeat(32)
    a = np.empty((k // 512, 16))
    for p in range(k // 512):
        a[p, :8] = np.random.permutation(np.resize(levels, 8))
        for g in range(8):
            far = levels[np.abs(levels - a[p, g]) >= 10]
            a[p, g + 8] = far[np.random.randint(len(far))]
    return np.exp2(a.ravel()).repeat(32)


def f64(x):
    return np.asarray(x).astype(np.float64)


def striped(idx):
    return np.tile(idx.reshape(-1, 16).T, (8, 1)).astype(np.uint16)


def unstriped(offs):
    return offs[:16].T.reshape(-1).astype(np.int64)


E2M1 = np.array([0.0, 0.5, 1.0, 1.5, 2.0, 3.0, 4.0, 6.0, -0.0, -0.5, -1.0, -1.5, -2.0, -3.0, -4.0, -6.0])


def pack_weight(w, fmt):
    k, n = w.shape
    w = f64(np.asarray(w, np.float32).astype(ml_dtypes.bfloat16)).reshape(k // 32, 32, n)
    amax = np.abs(w).max(1)
    if fmt == "e4m3":
        byte = np.frexp(amax)[1] - 1 + 127 - 7
    else:
        mant, ex = np.frexp(amax / 6.0)
        byte = np.where(mant > 0.5, ex, ex - 1) + 127
    byte = np.clip(np.where(amax > 0, byte, 1), 1, 254)
    scaled = (w * np.exp2(127.0 - byte)[:, None, :]).reshape(k, n).astype(np.float32)
    by_word = np.ascontiguousarray(scaled.reshape(k // 512, 128, 4, n).transpose(0, 1, 3, 2))
    if fmt == "e4m3":
        words = by_word.astype(ml_dtypes.float8_e4m3fn).view(np.uint8)
    else:
        c = by_word.astype(ml_dtypes.float4_e2m1fn).view(np.uint8) & 0xF
        words = (c[..., 0::2] | (c[..., 1::2] << 4)).reshape(k // 512, 128, 2 * n)
    return np.ascontiguousarray(words), np.ascontiguousarray(byte.astype(np.uint8).reshape(k // 512, 16, n))


def unpack_weight(words, scales, fmt):
    g, _, n = scales.shape
    words = np.ascontiguousarray(words).reshape(g, 128, n, -1)
    if fmt == "e4m3":
        vals = words.view(ml_dtypes.float8_e4m3fn).astype(np.float64)
    else:
        nib = np.empty((g, 128, n, 4), np.uint8)
        nib[..., 0::2] = words & 0xF
        nib[..., 1::2] = words >> 4
        vals = E2M1[nib]
    vals = vals * np.repeat(np.exp2(scales.astype(np.float64) - 127.0), 8, axis=1)[..., None]
    return vals.transpose(0, 1, 3, 2).reshape(g * 512, n)


def pack_table4(v):
    words, scales = pack_weight(v, "e2m1")
    g, t = words.shape[0] // 2, v.shape[1]
    words = words.reshape(g, 2, 128, t, 2).transpose(0, 2, 3, 1, 4)
    return np.concatenate([words.reshape(g, -1), scales.reshape(g, -1)], axis=1)


def unpack_table4(tab):
    g, t = tab.shape[0], tab.shape[1] // 544
    words = tab[:, :512 * t].reshape(g, 128, t, 2, 2).transpose(0, 3, 1, 2, 4).reshape(2 * g, 128, 2 * t)
    return unpack_weight(words, tab[:, 512 * t:].reshape(2 * g, 16, t), "e2m1")


def pack_table(v):
    words, scales = pack_weight(v, "e4m3")
    return np.concatenate([words.reshape(words.shape[0], -1), scales.reshape(scales.shape[0], -1)], axis=1)


def unpack_table(tab):
    g, t = tab.shape[0], tab.shape[1] // 528
    return unpack_weight(tab[:, :512 * t].reshape(g, 128, t, 4), tab[:, 512 * t:].reshape(g, 16, t), "e4m3")


K, L, M, T, S = 1536, 1024, 128, 1024, 512


def setup_inputs():
    n = np.random.standard_normal
    s1 = mx_kscale(K)[:, None]
    s2 = mx_kscale(L)[:, None]
    p_w4 = pack_weight(n((K, M)) / np.sqrt(K) / s1, "e2m1")
    return {
        "tab": pack_table(n((K, T)) * s1),
        "w4_words": p_w4[0],
        "w4_scales": p_w4[1],
        "tab2": pack_table4(n((L, T)) * s2),
        "u": (n((L, M)) / np.sqrt(L) / s2).astype(np.float32),
        "offs": striped(np.random.permutation(T)[:S]),
        "offs2": striped(np.random.permutation(T)[:S]),
    }


def reference(tab, w4_words, w4_scales, tab2, u, offs, offs2):
    tab_ = unpack_table(tab)[:, unstriped(offs)]
    w4_ = unpack_weight(w4_words, w4_scales, "e2m1")
    tab2_ = unpack_table4(tab2)[:, unstriped(offs2)]
    u_ = mxq(f64(u), 0, "e4m3")
    y = w4_.T @ tab_ + u_.T @ tab2_
    return y

@@ -1,0 +1,147 @@
+from contextlib import ExitStack
+
+import concourse.mybir as mybir
+
+F32 = mybir.dt.float32
+BF16 = mybir.dt.bfloat16
+I32 = mybir.dt.int32
+U32 = mybir.dt.uint32
+U16 = mybir.dt.uint16
+U8 = mybir.dt.uint8
+FP8X4 = mybir.dt.float8_e4m3fn_x4
+FP4X4 = mybir.dt.float4_e2m1fn_x4
+
+P = 128
+K, L, M, T, S = 1536, 1024, 128, 1024, 512
+KP = K // 512
+LP = L // 512
+QUAD = 32
+GROUP = 128
+GROUPS = S // GROUP
+FLOPS = 2 * M * S * (K + L)
+
+
+def tile_list_tab48_none_kernel(tc, tab, w4_words, w4_scales, tab2, u, offs, offs2, out):
+    nc = tc.nc
+    with ExitStack() as ctx:
+        keep = ctx.enter_context(tc.tile_pool(name="keep", bufs=1))
+        psum = ctx.enter_context(tc.psum_pool(name="psum", bufs=1))
+
+        list1 = keep.tile([P, S // 16], U16, name="list1")
+        list2 = keep.tile([P, S // 16], U16, name="list2")
+        sc2 = keep.tile([P, T // 4], I32, name="sc2", align_bytes=64)
+        sc1 = keep.tile([P, KP * T // 4 + 16], I32, name="sc1", tag="turns", align_bytes=64)
+        zero = keep.tile([P, 1], I32, name="zero", tag="zeros", align_bytes=64)
+        words2 = keep.tile([P, T], I32, name="words2", align_bytes=64)
+        words1 = [keep.tile([P, T], I32, name=f"words1_{a}", align_bytes=64) for a in range(KP)]
+        u_raw = keep.tile([P, LP, 4, M], F32, name="u_raw", align_bytes=64)
+        u_bf = keep.tile([P, LP, M, 4], BF16, name="u_bf", align_bytes=64)
+        u_scales = keep.tile([P, LP * M], U8, name="u_scales", align_bytes=64)
+        w_words = keep.tile([P, KP, 2 * M], U8, name="w_words", align_bytes=64)
+        g_words2 = keep.tile([P, S], U32, name="g_words2", align_bytes=64)
+        parted2 = keep.tile([P, LP * 2 * S], U8, name="parted2", align_bytes=64)
+        g_sc2 = keep.tile([P, S], U8, name="g_sc2", align_bytes=64)
+        shifted2 = keep.tile([P, S // 4], I32, name="shifted2", align_bytes=64)
+        g_words1 = [keep.tile([P, S], U32, name=f"g_words1_{a}", align_bytes=64) for a in range(KP)]
+        g_sc1 = [keep.tile([P, S], U8, name=f"g_sc1_{a}", align_bytes=64) for a in range(KP)]
+        out_a = keep.tile([P, S - GROUP], F32, name="out_a", align_bytes=64)
+        out_b = keep.tile([P, GROUP], F32, name="out_b", align_bytes=64)
+        banks = [psum.tile([P, 512], F32, name=f"bank{g}") for g in range(GROUPS)]
+
+        nc.gpsimd.memset(shifted2[:], 0)
+        nc.vector.memset(sc1[:], 0)
+        nc.gpsimd.memset(words2[:, 0:1], 0)
+        nc.vector.tensor_copy(zero[:], sc1[:, KP * T // 4 : KP * T // 4 + 1])
+        for a in range(KP):
+            nc.vector.tensor_copy(words1[a][:, 0:1], zero[:])
+        w_sc = keep.tile([P, KP, M // 4], I32, name="w_sc", tag="zeros", align_bytes=64)
+        nc.vector.memset(w_sc[:], 0)
+
+        def load_words(eng, tile, src):
+            eng.dma_start(tile[:], src[0 : 512 * T].rearrange("(p b) -> p b", p=P).bitcast(I32))
+
+        nc.sync.dma_start(list2[:], offs2)
+        tab2_sc = tab2[0, 512 * T :].rearrange("(r t) -> r t", t=T).bitcast(I32)
+        nc.sync.dma_start(sc2[0:QUAD, :], tab2_sc)
+        for q in range(1, 4):
+            rows = tab2_sc[4 * q : 4 * q + 4, :].unsqueeze(0).to_broadcast([8, 4, T // 4])
+            nc.sync.dma_start(sc2[QUAD * q : QUAD * (q + 1), :], rows)
+        load_words(nc.sync, words2, tab2[0])
+        nc.sync.dma_start(list1[:], offs)
+        nc.gpsimd.dma_start(u_raw[:].rearrange("p h j n -> p h (j n)"), u.rearrange("(h p j) n -> p h (j n)", h=LP, j=4))
+        nc.gpsimd.dma_start(w_words[:].bitcast(I32), w4_words.rearrange("a p b -> p a b").bitcast(I32))
+        tab_sc = tab[:, 512 * T :].rearrange("a (q t) -> q a t", q=16)
+        sc1_planes = sc1[:, 0 : KP * T // 4].rearrange("p (a t) -> p a t", a=KP)
+        for q in range(4):
+            nc.sync.dma_start(sc1_planes[QUAD * q : QUAD * q + 4, :, :], tab_sc[4 * q : 4 * q + 4].bitcast(I32))
+        for a in range(KP):
+            load_words(nc.sync, words1[a], tab[a])
+        w_sc_src = w4_scales.rearrange("a q n -> q a n")
+        for q in range(4):
+            nc.sync.dma_start(w_sc[QUAD * q : QUAD * q + 4, :, :], w_sc_src[4 * q : 4 * q + 4].bitcast(I32))
+
+        nc.scalar.copy(u_bf[:], u_raw[:].rearrange("p h j n -> p h n j"))
+
+        nc.vector.tensor_copy(g_sc2[:], sc2[:].bitcast(U8).indirect(list2[:]))
+        for q in range(4):
+            nc.scalar.dma_start(shifted2[QUAD * q : QUAD * q + 4, :], g_sc2[16 + 4 * q : 20 + 4 * q, :].bitcast(I32))
+        nc.vector.tensor_copy(g_words2[:], words2[:].bitcast(U32).indirect(list2[:]))
+        nc.vector.tensor_copy(
+            parted2[:].bitcast(U16).rearrange("p (h n) -> p h n", h=LP),
+            g_words2[:].bitcast(U16).rearrange("p (n h) -> p h n", h=LP),
+        )
+        sc1_u8 = sc1[:].bitcast(U8)
+        for a in range(KP):
+            nc.vector.tensor_copy(g_sc1[a][:], sc1_u8[:, T * a : T * (a + 1)].indirect(list1[:]))
+        u_codes = keep.tile([P, LP * M], U32, name="u_codes", tag="turns", align_bytes=64)
+        nc.vector.quantize_mx(
+            out=u_codes[:].bitcast(FP8X4),
+            scales=u_scales[:],
+            in_=u_bf[:].rearrange("p h n j -> p (h n j)"),
+        )
+        shifted2_u8 = shifted2[:].bitcast(U8)
+        w_sc_u8 = w_sc[:].rearrange("p a n -> p (a n)").bitcast(U8)
+
+        def multiply2(h):
+            plane = (g_sc2[:], shifted2_u8)[h]
+            for g in range(GROUPS):
+                nc.tensor.matmul_mx(
+                    out=banks[g][:, 0:GROUP],
+                    lhsT=u_codes[:, M * h : M * (h + 1)].bitcast(FP8X4),
+                    lhsT_scale=u_scales[:, M * h : M * (h + 1)],
+                    rhs=parted2[:, 2 * S * h + 2 * GROUP * g : 2 * S * h + 2 * GROUP * (g + 1)].bitcast(FP4X4),
+                    rhs_scale=plane[:, GROUP * g : GROUP * (g + 1)],
+                    start=(h == 0),
+                    stop=False,
+                )
+
+        def gather_and_multiply(a, pieces):
+            done = 0
+            for piece in pieces:
+                nc.vector.tensor_copy(
+                    g_words1[a][:, done : done + piece],
+                    words1[a][:].bitcast(U32).indirect(list1[:, done // 16 : (done + piece) // 16]),
+                )
+                for g in range(done // GROUP, (done + piece) // GROUP):
+                    nc.tensor.matmul_mx(
+                        out=banks[g][:, 0:GROUP],
+                        lhsT=w_words[:, a, :].bitcast(FP4X4),
+                        lhsT_scale=w_sc_u8[:, M * a : M * (a + 1)],
+                        rhs=g_words1[a][:, GROUP * g : GROUP * (g + 1)].bitcast(FP8X4),
+                        rhs_scale=g_sc1[a][:, GROUP * g : GROUP * (g + 1)],
+                        start=False,
+                        stop=(a == KP - 1),
+                    )
+                done += piece
+
+        multiply2(0)
+        gather_and_multiply(0, (S,))
+        multiply2(1)
+        gather_and_multiply(1, (S,))
+        gather_and_multiply(2, (2 * GROUP, GROUP, GROUP))
+        cut = S - GROUP
+        for g in range(GROUPS - 1):
+            nc.scalar.copy(out_a[:, GROUP * g : GROUP * (g + 1)], banks[g][:, 0:GROUP])
+        nc.sync.dma_start(out[:, 0:cut], out_a[:])
+        nc.vector.tensor_copy(out_b[:], banks[GROUPS - 1][:, 0:GROUP])
+        nc.scalar.dma_start(out[:, cut:S], out_b[:])

@@ -29,81 +29,76 @@ def tile_list_tab48_none_kernel(tc, tab, w4_words, w4_scales, tab2, u, offs, off
 
         list1 = keep.tile([P, S // 16], U16, name="list1")
         list2 = keep.tile([P, S // 16], U16, name="list2")
-        sc2 = keep.tile([P, T // 4], I32, name="sc2", align_bytes=64)
-        sc1 = keep.tile([P, KP * T // 4 + 16], I32, name="sc1", tag="turns", align_bytes=64)
-        zero = keep.tile([P, 1], I32, name="zero", tag="zeros", align_bytes=64)
+        rows1 = keep.tile([P, T // 4], I32, name="rows1", align_bytes=64)
+        rows2 = keep.tile([P, T // 4], I32, name="rows2", align_bytes=64)
         words2 = keep.tile([P, T], I32, name="words2", align_bytes=64)
         words1 = [keep.tile([P, T], I32, name=f"words1_{a}", align_bytes=64) for a in range(KP)]
         u_raw = keep.tile([P, LP, 4, M], F32, name="u_raw", align_bytes=64)
         u_bf = keep.tile([P, LP, M, 4], BF16, name="u_bf", align_bytes=64)
+        u_codes = keep.tile([P, LP * M], U32, name="u_codes", align_bytes=64)
         u_scales = keep.tile([P, LP * M], U8, name="u_scales", align_bytes=64)
         w_words = keep.tile([P, KP, 2 * M], U8, name="w_words", align_bytes=64)
+        w_sc = keep.tile([P, KP, M // 4], I32, name="w_sc", align_bytes=64)
         g_words2 = keep.tile([P, S], U32, name="g_words2", align_bytes=64)
         parted2 = keep.tile([P, LP * 2 * S], U8, name="parted2", align_bytes=64)
-        g_sc2 = keep.tile([P, S], U8, name="g_sc2", align_bytes=64)
-        shifted2 = keep.tile([P, S // 4], I32, name="shifted2", align_bytes=64)
+        g_rows = keep.tile([P, 2 * S], U8, name="g_rows", align_bytes=64)
+        planes = keep.tile([P, 4 * S // 4], I32, name="planes", align_bytes=64)
+        plane_last = keep.tile([P, S // 4], I32, name="plane_last", align_bytes=64)
         g_words1 = [keep.tile([P, S], U32, name=f"g_words1_{a}", align_bytes=64) for a in range(KP)]
-        g_sc1 = [keep.tile([P, S], U8, name=f"g_sc1_{a}", align_bytes=64) for a in range(KP)]
         out_a = keep.tile([P, S - GROUP], F32, name="out_a", align_bytes=64)
         out_b = keep.tile([P, GROUP], F32, name="out_b", align_bytes=64)
         banks = [psum.tile([P, 512], F32, name=f"bank{g}") for g in range(GROUPS)]
 
-        nc.gpsimd.memset(shifted2[:], 0)
-        nc.vector.memset(sc1[:], 0)
-        nc.gpsimd.memset(words2[:, 0:1], 0)
-        nc.vector.tensor_copy(zero[:], sc1[:, KP * T // 4 : KP * T // 4 + 1])
-        for a in range(KP):
-            nc.vector.tensor_copy(words1[a][:, 0:1], zero[:])
-        w_sc = keep.tile([P, KP, M // 4], I32, name="w_sc", tag="zeros", align_bytes=64)
-        nc.vector.memset(w_sc[:], 0)
+        nc.gpsimd.memset(w_sc[:], 0)
+        nc.vector.memset(rows2[0:96, :], 0)
+        nc.vector.memset(rows1[0:80, :], 0)
+        nc.vector.memset(planes[:], 0)
+        nc.vector.memset(plane_last[:], 0)
 
         def load_words(eng, tile, src):
             eng.dma_start(tile[:], src[0 : 512 * T].rearrange("(p b) -> p b", p=P).bitcast(I32))
 
         nc.sync.dma_start(list2[:], offs2)
-        tab2_sc = tab2[0, 512 * T :].rearrange("(r t) -> r t", t=T).bitcast(I32)
-        nc.sync.dma_start(sc2[0:QUAD, :], tab2_sc)
-        for q in range(1, 4):
-            rows = tab2_sc[4 * q : 4 * q + 4, :].unsqueeze(0).to_broadcast([8, 4, T // 4])
-            nc.sync.dma_start(sc2[QUAD * q : QUAD * (q + 1), :], rows)
-        load_words(nc.sync, words2, tab2[0])
+        nc.sync.dma_start(rows2[96:128, :], tab2[0, 512 * T :].rearrange("(h q t) -> q h t", h=LP, t=T).bitcast(I32))
         nc.sync.dma_start(list1[:], offs)
-        nc.gpsimd.dma_start(u_raw[:].rearrange("p h j n -> p h (j n)"), u.rearrange("(h p j) n -> p h (j n)", h=LP, j=4))
-        nc.gpsimd.dma_start(w_words[:].bitcast(I32), w4_words.rearrange("a p b -> p a b").bitcast(I32))
-        tab_sc = tab[:, 512 * T :].rearrange("a (q t) -> q a t", q=16)
-        sc1_planes = sc1[:, 0 : KP * T // 4].rearrange("p (a t) -> p a t", a=KP)
-        for q in range(4):
-            nc.sync.dma_start(sc1_planes[QUAD * q : QUAD * q + 4, :, :], tab_sc[4 * q : 4 * q + 4].bitcast(I32))
-        for a in range(KP):
+        tab_sc = tab[:, 512 * T :].rearrange("a (q t) -> q a t", q=16).bitcast(I32)
+        nc.sync.dma_start(rows1[96:128, :], tab_sc[:, 0:2, :])
+        nc.sync.dma_start(rows1[80:96, :], tab_sc[:, 2, :])
+        load_words(nc.sync, words2, tab2[0])
+        load_words(nc.sync, words1[0], tab[0])
+        nc.sync.dma_start(u_raw[:].rearrange("p h j n -> p h (j n)"), u.rearrange("(h p j) n -> p h (j n)", h=LP, j=4))
+        for a in range(1, KP):
             load_words(nc.sync, words1[a], tab[a])
+        nc.gpsimd.dma_start(w_words[:].bitcast(I32), w4_words.rearrange("a p b -> p a b").bitcast(I32))
         w_sc_src = w4_scales.rearrange("a q n -> q a n")
         for q in range(4):
-            nc.sync.dma_start(w_sc[QUAD * q : QUAD * q + 4, :, :], w_sc_src[4 * q : 4 * q + 4].bitcast(I32))
+            nc.gpsimd.dma_start(w_sc[QUAD * q : QUAD * q + 4, :, :], w_sc_src[4 * q : 4 * q + 4].bitcast(I32))
 
         nc.scalar.copy(u_bf[:], u_raw[:].rearrange("p h j n -> p h n j"))
 
-        nc.vector.tensor_copy(g_sc2[:], sc2[:].bitcast(U8).indirect(list2[:]))
+        nc.vector.tensor_copy(g_rows[:, S : 2 * S], rows2[:].bitcast(U8).indirect(list2[:]))
+        nc.vector.tensor_copy(g_rows[:, 0:S], rows1[:].bitcast(U8).indirect(list1[:]))
         for q in range(4):
-            nc.scalar.dma_start(shifted2[QUAD * q : QUAD * q + 4, :], g_sc2[16 + 4 * q : 20 + 4 * q, :].bitcast(I32))
+            nc.sync.dma_start(planes[QUAD * q : QUAD * q + 4, :], g_rows[96 + 8 * q : 104 + 8 * q, :].bitcast(I32))
+        for q in range(4):
+            nc.sync.dma_start(plane_last[QUAD * q : QUAD * q + 4, :], g_rows[80 + 4 * q : 84 + 4 * q, 0:S].bitcast(I32))
         nc.vector.tensor_copy(g_words2[:], words2[:].bitcast(U32).indirect(list2[:]))
         nc.vector.tensor_copy(
             parted2[:].bitcast(U16).rearrange("p (h n) -> p h n", h=LP),
             g_words2[:].bitcast(U16).rearrange("p (n h) -> p h n", h=LP),
         )
-        sc1_u8 = sc1[:].bitcast(U8)
-        for a in range(KP):
-            nc.vector.tensor_copy(g_sc1[a][:], sc1_u8[:, T * a : T * (a + 1)].indirect(list1[:]))
-        u_codes = keep.tile([P, LP * M], U32, name="u_codes", tag="turns", align_bytes=64)
         nc.vector.quantize_mx(
             out=u_codes[:].bitcast(FP8X4),
             scales=u_scales[:],
             in_=u_bf[:].rearrange("p h n j -> p (h n j)"),
         )
-        shifted2_u8 = shifted2[:].bitcast(U8)
+        planes_u8 = planes[:].bitcast(U8)
+        planes1 = [planes_u8[:, 0:S], planes_u8[:, 2 * S : 3 * S], plane_last[:].bitcast(U8)]
+        planes2 = [planes_u8[:, S : 2 * S], planes_u8[:, 3 * S : 4 * S]]
         w_sc_u8 = w_sc[:].rearrange("p a n -> p (a n)").bitcast(U8)
 
         def multiply2(h):
-            plane = (g_sc2[:], shifted2_u8)[h]
+            plane = planes2[h]
             for g in range(GROUPS):
                 nc.tensor.matmul_mx(
                     out=banks[g][:, 0:GROUP],
@@ -128,15 +123,15 @@ def tile_list_tab48_none_kernel(tc, tab, w4_words, w4_scales, tab2, u, offs, off
                         lhsT=w_words[:, a, :].bitcast(FP4X4),
                         lhsT_scale=w_sc_u8[:, M * a : M * (a + 1)],
                         rhs=g_words1[a][:, GROUP * g : GROUP * (g + 1)].bitcast(FP8X4),
-                        rhs_scale=g_sc1[a][:, GROUP * g : GROUP * (g + 1)],
+                        rhs_scale=planes1[a][:, GROUP * g : GROUP * (g + 1)],
                         start=False,
                         stop=(a == KP - 1),
                     )
                 done += piece
 
         multiply2(0)
-        gather_and_multiply(0, (S,))
         multiply2(1)
+        gather_and_multiply(0, (S,))
         gather_and_multiply(1, (S,))
         gather_and_multiply(2, (2 * GROUP, GROUP, GROUP))
         cut = S - GROUP

@@ -29,10 +29,10 @@ def tile_list_tab48_none_kernel(tc, tab, w4_words, w4_scales, tab2, u, offs, off
 
         list1 = keep.tile([P, S // 16], U16, name="list1")
         list2 = keep.tile([P, S // 16], U16, name="list2")
-        rows1 = keep.tile([P, T // 4], I32, name="rows1", align_bytes=64)
+        rows1 = keep.tile([P, T // 4], I32, name="rows1", tag="turns", align_bytes=64)
         rows2 = keep.tile([P, T // 4], I32, name="rows2", align_bytes=64)
         words2 = keep.tile([P, T], I32, name="words2", align_bytes=64)
-        words1 = [keep.tile([P, T], I32, name=f"words1_{a}", align_bytes=64) for a in range(KP)]
+        words1 = [keep.tile([P, T], I32, name=f"words1_{a}", align_bytes=64) for a in range(KP - 1)]
         u_raw = keep.tile([P, LP, 4, M], F32, name="u_raw", align_bytes=64)
         u_bf = keep.tile([P, LP, M, 4], BF16, name="u_bf", align_bytes=64)
         u_codes = keep.tile([P, LP * M], U32, name="u_codes", align_bytes=64)
@@ -64,11 +64,10 @@ def tile_list_tab48_none_kernel(tc, tab, w4_words, w4_scales, tab2, u, offs, off
         tab_sc = tab[:, 512 * T :].rearrange("a (q t) -> q a t", q=16).bitcast(I32)
         nc.sync.dma_start(rows1[96:128, :], tab_sc[:, 0:2, :])
         nc.sync.dma_start(rows1[80:96, :], tab_sc[:, 2, :])
+        nc.sync.dma_start(u_raw[:].rearrange("p h j n -> p h (j n)"), u.rearrange("(h p j) n -> p h (j n)", h=LP, j=4))
         load_words(nc.sync, words2, tab2[0])
         load_words(nc.sync, words1[0], tab[0])
-        nc.sync.dma_start(u_raw[:].rearrange("p h j n -> p h (j n)"), u.rearrange("(h p j) n -> p h (j n)", h=LP, j=4))
-        for a in range(1, KP):
-            load_words(nc.sync, words1[a], tab[a])
+        load_words(nc.sync, words1[1], tab[1])
         nc.gpsimd.dma_start(w_words[:].bitcast(I32), w4_words.rearrange("a p b -> p a b").bitcast(I32))
         w_sc_src = w4_scales.rearrange("a q n -> q a n")
         for q in range(4):
@@ -80,6 +79,8 @@ def tile_list_tab48_none_kernel(tc, tab, w4_words, w4_scales, tab2, u, offs, off
         nc.vector.tensor_copy(g_rows[:, 0:S], rows1[:].bitcast(U8).indirect(list1[:]))
         for q in range(4):
             nc.sync.dma_start(planes[QUAD * q : QUAD * q + 4, :], g_rows[96 + 8 * q : 104 + 8 * q, :].bitcast(I32))
+        words1.append(keep.tile([P, T], I32, name="words1_last", tag="turns", align_bytes=64))
+        load_words(nc.sync, words1[2], tab[2])
         for q in range(4):
             nc.sync.dma_start(plane_last[QUAD * q : QUAD * q + 4, :], g_rows[80 + 4 * q : 84 + 4 * q, 0:S].bitcast(I32))
         nc.vector.tensor_copy(g_words2[:], words2[:].bitcast(U32).indirect(list2[:]))

@@ -33,14 +33,13 @@ def tile_list_tab48_none_kernel(tc, tab, w4_words, w4_scales, tab2, u, offs, off
         rows2 = keep.tile([P, T // 4], I32, name="rows2", align_bytes=64)
         words2 = keep.tile([P, T], I32, name="words2", align_bytes=64)
         words1 = [keep.tile([P, T], I32, name=f"words1_{a}", align_bytes=64) for a in range(KP - 1)]
-        u_raw = keep.tile([P, LP, 4, M], F32, name="u_raw", align_bytes=64)
+        u_raw = keep.tile([P, LP, 4, M], F32, name="u_raw", tag="staged", align_bytes=64)
         u_bf = keep.tile([P, LP, M, 4], BF16, name="u_bf", align_bytes=64)
         u_codes = keep.tile([P, LP * M], U32, name="u_codes", align_bytes=64)
         u_scales = keep.tile([P, LP * M], U8, name="u_scales", align_bytes=64)
         w_words = keep.tile([P, KP, 2 * M], U8, name="w_words", align_bytes=64)
         w_sc = keep.tile([P, KP, M // 4], I32, name="w_sc", align_bytes=64)
         g_words2 = keep.tile([P, S], U32, name="g_words2", align_bytes=64)
-        parted2 = keep.tile([P, LP * 2 * S], U8, name="parted2", align_bytes=64)
         g_rows = keep.tile([P, 2 * S], U8, name="g_rows", align_bytes=64)
         planes = keep.tile([P, 4 * S // 4], I32, name="planes", align_bytes=64)
         plane_last = keep.tile([P, S // 4], I32, name="plane_last", align_bytes=64)
@@ -84,14 +83,15 @@ def tile_list_tab48_none_kernel(tc, tab, w4_words, w4_scales, tab2, u, offs, off
         for q in range(4):
             nc.sync.dma_start(plane_last[QUAD * q : QUAD * q + 4, :], g_rows[80 + 4 * q : 84 + 4 * q, 0:S].bitcast(I32))
         nc.vector.tensor_copy(g_words2[:], words2[:].bitcast(U32).indirect(list2[:]))
-        nc.vector.tensor_copy(
-            parted2[:].bitcast(U16).rearrange("p (h n) -> p h n", h=LP),
-            g_words2[:].bitcast(U16).rearrange("p (n h) -> p h n", h=LP),
-        )
         nc.vector.quantize_mx(
             out=u_codes[:].bitcast(FP8X4),
             scales=u_scales[:],
             in_=u_bf[:].rearrange("p h n j -> p (h n j)"),
+        )
+        parted2 = keep.tile([P, LP * 2 * S], U8, name="parted2", tag="staged", align_bytes=64)
+        nc.vector.tensor_copy(
+            parted2[:].bitcast(U16).rearrange("p (h n) -> p h n", h=LP),
+            g_words2[:].bitcast(U16).rearrange("p (n h) -> p h n", h=LP),
         )
         planes_u8 = planes[:].bitcast(U8)
         planes1 = [planes_u8[:, 0:S], planes_u8[:, 2 * S : 3 * S], plane_last[:].bitcast(U8)]

@@ -58,11 +58,11 @@ def tile_list_tab48_none_kernel(tc, tab, w4_words, w4_scales, tab2, u, offs, off
             eng.dma_start(tile[:], src[0 : 512 * T].rearrange("(p b) -> p b", p=P).bitcast(I32))
 
         nc.sync.dma_start(list2[:], offs2)
-        nc.sync.dma_start(rows2[96:128, :], tab2[0, 512 * T :].rearrange("(h q t) -> q h t", h=LP, t=T).bitcast(I32))
+        nc.scalar.dma_start(rows2[96:128, :], tab2[0, 512 * T :].rearrange("(h q t) -> q h t", h=LP, t=T).bitcast(I32))
         nc.sync.dma_start(list1[:], offs)
         tab_sc = tab[:, 512 * T :].rearrange("a (q t) -> q a t", q=16).bitcast(I32)
-        nc.sync.dma_start(rows1[96:128, :], tab_sc[:, 0:2, :])
-        nc.sync.dma_start(rows1[80:96, :], tab_sc[:, 2, :])
+        nc.scalar.dma_start(rows1[96:128, :], tab_sc[:, 0:2, :])
+        nc.scalar.dma_start(rows1[80:96, :], tab_sc[:, 2, :])
         nc.sync.dma_start(u_raw[:].rearrange("p h j n -> p h (j n)"), u.rearrange("(h p j) n -> p h (j n)", h=LP, j=4))
         load_words(nc.sync, words2, tab2[0])
         load_words(nc.sync, words1[0], tab[0])

@@ -48,11 +48,8 @@ def tile_list_tab48_none_kernel(tc, tab, w4_words, w4_scales, tab2, u, offs, off
         out_b = keep.tile([P, GROUP], F32, name="out_b", align_bytes=64)
         banks = [psum.tile([P, 512], F32, name=f"bank{g}") for g in range(GROUPS)]
 
-        nc.gpsimd.memset(w_sc[:], 0)
         nc.vector.memset(rows2[0:96, :], 0)
         nc.vector.memset(rows1[0:80, :], 0)
-        nc.vector.memset(planes[:], 0)
-        nc.vector.memset(plane_last[:], 0)
 
         def load_words(eng, tile, src):
             eng.dma_start(tile[:], src[0 : 512 * T].rearrange("(p b) -> p b", p=P).bitcast(I32))
@@ -67,10 +64,10 @@ def tile_list_tab48_none_kernel(tc, tab, w4_words, w4_scales, tab2, u, offs, off
         load_words(nc.sync, words2, tab2[0])
         load_words(nc.sync, words1[0], tab[0])
         load_words(nc.sync, words1[1], tab[1])
-        nc.gpsimd.dma_start(w_words[:].bitcast(I32), w4_words.rearrange("a p b -> p a b").bitcast(I32))
         w_sc_src = w4_scales.rearrange("a q n -> q a n")
         for q in range(4):
             nc.gpsimd.dma_start(w_sc[QUAD * q : QUAD * q + 4, :, :], w_sc_src[4 * q : 4 * q + 4].bitcast(I32))
+        nc.gpsimd.dma_start(w_words[:].bitcast(I32), w4_words.rearrange("a p b -> p a b").bitcast(I32))
 
         nc.scalar.copy(u_bf[:], u_raw[:].rearrange("p h j n -> p h n j"))
 

@@ -44,8 +44,8 @@ def tile_list_tab48_none_kernel(tc, tab, w4_words, w4_scales, tab2, u, offs, off
         planes = keep.tile([P, 4 * S // 4], I32, name="planes", align_bytes=64)
         plane_last = keep.tile([P, S // 4], I32, name="plane_last", align_bytes=64)
         g_words1 = [keep.tile([P, S], U32, name=f"g_words1_{a}", align_bytes=64) for a in range(KP)]
-        out_a = keep.tile([P, S - GROUP], F32, name="out_a", align_bytes=64)
-        out_b = keep.tile([P, GROUP], F32, name="out_b", align_bytes=64)
+        out_a = keep.tile([P, 2 * GROUP], F32, name="out_a", align_bytes=64)
+        out_b = keep.tile([P, 2 * GROUP], F32, name="out_b", align_bytes=64)
         banks = [psum.tile([P, 512], F32, name=f"bank{g}") for g in range(GROUPS)]
 
         nc.vector.memset(rows2[0:96, :], 0)
@@ -132,9 +132,9 @@ def tile_list_tab48_none_kernel(tc, tab, w4_words, w4_scales, tab2, u, offs, off
         gather_and_multiply(0, (S,))
         gather_and_multiply(1, (S,))
         gather_and_multiply(2, (2 * GROUP, GROUP, GROUP))
-        cut = S - GROUP
-        for g in range(GROUPS - 1):
+        for g in range(2):
             nc.scalar.copy(out_a[:, GROUP * g : GROUP * (g + 1)], banks[g][:, 0:GROUP])
-        nc.sync.dma_start(out[:, 0:cut], out_a[:])
-        nc.vector.tensor_copy(out_b[:], banks[GROUPS - 1][:, 0:GROUP])
-        nc.scalar.dma_start(out[:, cut:S], out_b[:])
+        nc.sync.dma_start(out[:, 0 : 2 * GROUP], out_a[:])
+        nc.scalar.copy(out_b[:, 0:GROUP], banks[2][:, 0:GROUP])
+        nc.vector.tensor_copy(out_b[:, GROUP : 2 * GROUP], banks[3][:, 0:GROUP])
+        nc.scalar.dma_start(out[:, 2 * GROUP : S], out_b[:])

@@ -25,15 +25,16 @@ def tile_list_tab48_none_kernel(tc, tab, w4_words, w4_scales, tab2, u, offs, off
     nc = tc.nc
     with ExitStack() as ctx:
         keep = ctx.enter_context(tc.tile_pool(name="keep", bufs=1))
+        staged = ctx.enter_context(tc.tile_pool(name="staged", bufs=1))
         psum = ctx.enter_context(tc.psum_pool(name="psum", bufs=1))
 
         list1 = keep.tile([P, S // 16], U16, name="list1")
         list2 = keep.tile([P, S // 16], U16, name="list2")
         rows1 = keep.tile([P, T // 4], I32, name="rows1", tag="turns", align_bytes=64)
-        rows2 = keep.tile([P, T // 4], I32, name="rows2", align_bytes=64)
+        rows2 = keep.tile([P, T // 4], I32, name="rows2", tag="turns2", align_bytes=64)
         words2 = keep.tile([P, T], I32, name="words2", align_bytes=64)
-        words1 = [keep.tile([P, T], I32, name=f"words1_{a}", align_bytes=64) for a in range(KP - 1)]
-        u_raw = keep.tile([P, LP, 4, M], F32, name="u_raw", tag="staged", align_bytes=64)
+        words1 = [keep.tile([P, T], I32, name="words1_0", align_bytes=64)]
+        u_raw = staged.tile([P, LP, 4, M], F32, name="u_raw", offset=0, align_bytes=64)
         u_bf = keep.tile([P, LP, M, 4], BF16, name="u_bf", align_bytes=64)
         u_codes = keep.tile([P, LP * M], U32, name="u_codes", align_bytes=64)
         u_scales = keep.tile([P, LP * M], U8, name="u_scales", align_bytes=64)
@@ -41,9 +42,11 @@ def tile_list_tab48_none_kernel(tc, tab, w4_words, w4_scales, tab2, u, offs, off
         w_sc = keep.tile([P, KP, M // 4], I32, name="w_sc", align_bytes=64)
         g_words2 = keep.tile([P, S], U32, name="g_words2", align_bytes=64)
         g_rows = keep.tile([P, 2 * S], U8, name="g_rows", align_bytes=64)
-        planes = keep.tile([P, 4 * S // 4], I32, name="planes", align_bytes=64)
+        planes_tab = keep.tile([P, 2 * S // 4], I32, name="planes_tab", align_bytes=64)
+        planes_tab2 = keep.tile([P, 2 * S // 4], I32, name="planes_tab2", align_bytes=64)
         plane_last = keep.tile([P, S // 4], I32, name="plane_last", align_bytes=64)
-        g_words1 = [keep.tile([P, S], U32, name=f"g_words1_{a}", align_bytes=64) for a in range(KP)]
+        g_words1 = [staged.tile([P, S], U32, name="g_words1_0", offset=4 * S, align_bytes=64)]
+        g_words1 += [keep.tile([P, S], U32, name=f"g_words1_{a}", align_bytes=64) for a in range(1, KP)]
         out_a = keep.tile([P, 2 * GROUP], F32, name="out_a", align_bytes=64)
         out_b = keep.tile([P, 2 * GROUP], F32, name="out_b", align_bytes=64)
         banks = [psum.tile([P, 512], F32, name=f"bank{g}") for g in range(GROUPS)]
@@ -63,7 +66,6 @@ def tile_list_tab48_none_kernel(tc, tab, w4_words, w4_scales, tab2, u, offs, off
         nc.sync.dma_start(u_raw[:].rearrange("p h j n -> p h (j n)"), u.rearrange("(h p j) n -> p h (j n)", h=LP, j=4))
         load_words(nc.sync, words2, tab2[0])
         load_words(nc.sync, words1[0], tab[0])
-        load_words(nc.sync, words1[1], tab[1])
         w_sc_src = w4_scales.rearrange("a q n -> q a n")
         for q in range(4):
             nc.gpsimd.dma_start(w_sc[QUAD * q : QUAD * q + 4, :, :], w_sc_src[4 * q : 4 * q + 4].bitcast(I32))
@@ -72,9 +74,13 @@ def tile_list_tab48_none_kernel(tc, tab, w4_words, w4_scales, tab2, u, offs, off
         nc.scalar.copy(u_bf[:], u_raw[:].rearrange("p h j n -> p h n j"))
 
         nc.vector.tensor_copy(g_rows[:, S : 2 * S], rows2[:].bitcast(U8).indirect(list2[:]))
+        for q in range(4):
+            nc.sync.dma_start(planes_tab2[QUAD * q : QUAD * q + 4, :], g_rows[96 + 8 * q : 104 + 8 * q, S : 2 * S].bitcast(I32))
+        words1.append(keep.tile([P, T], I32, name="words1_1", tag="turns2", align_bytes=64))
+        load_words(nc.sync, words1[1], tab[1])
         nc.vector.tensor_copy(g_rows[:, 0:S], rows1[:].bitcast(U8).indirect(list1[:]))
         for q in range(4):
-            nc.sync.dma_start(planes[QUAD * q : QUAD * q + 4, :], g_rows[96 + 8 * q : 104 + 8 * q, :].bitcast(I32))
+            nc.sync.dma_start(planes_tab[QUAD * q : QUAD * q + 4, :], g_rows[96 + 8 * q : 104 + 8 * q, 0:S].bitcast(I32))
         words1.append(keep.tile([P, T], I32, name="words1_last", tag="turns", align_bytes=64))
         load_words(nc.sync, words1[2], tab[2])
         for q in range(4):
@@ -85,14 +91,13 @@ def tile_list_tab48_none_kernel(tc, tab, w4_words, w4_scales, tab2, u, offs, off
             scales=u_scales[:],
             in_=u_bf[:].rearrange("p h n j -> p (h n j)"),
         )
-        parted2 = keep.tile([P, LP * 2 * S], U8, name="parted2", tag="staged", align_bytes=64)
+        parted2 = staged.tile([P, LP * 2 * S], U8, name="parted2", offset=0, align_bytes=64)
         nc.vector.tensor_copy(
             parted2[:].bitcast(U16).rearrange("p (h n) -> p h n", h=LP),
             g_words2[:].bitcast(U16).rearrange("p (n h) -> p h n", h=LP),
         )
-        planes_u8 = planes[:].bitcast(U8)
-        planes1 = [planes_u8[:, 0:S], planes_u8[:, 2 * S : 3 * S], plane_last[:].bitcast(U8)]
-        planes2 = [planes_u8[:, S : 2 * S], planes_u8[:, 3 * S : 4 * S]]
+        planes1 = [planes_tab[:].bitcast(U8)[:, S * a : S * (a + 1)] for a in range(KP - 1)] + [plane_last[:].bitcast(U8)]
+        planes2 = [planes_tab2[:].bitcast(U8)[:, S * h : S * (h + 1)] for h in range(LP)]
         w_sc_u8 = w_sc[:].rearrange("p a n -> p (a n)").bitcast(U8)
 
         def multiply2(h):

@@ -44,7 +44,7 @@ def tile_list_tab48_none_kernel(tc, tab, w4_words, w4_scales, tab2, u, offs, off
         g_rows = keep.tile([P, 2 * S], U8, name="g_rows", align_bytes=64)
         planes_tab = keep.tile([P, 2 * S // 4], I32, name="planes_tab", align_bytes=64)
         planes_tab2 = keep.tile([P, 2 * S // 4], I32, name="planes_tab2", align_bytes=64)
-        plane_last = keep.tile([P, S // 4], I32, name="plane_last", align_bytes=64)
+        plane_first = keep.tile([P, S // 4], I32, name="plane_first", align_bytes=64)
         g_words1 = [staged.tile([P, S], U32, name="g_words1_0", offset=4 * S, align_bytes=64)]
         g_words1 += [keep.tile([P, S], U32, name=f"g_words1_{a}", align_bytes=64) for a in range(1, KP)]
         out_a = keep.tile([P, 2 * GROUP], F32, name="out_a", align_bytes=64)
@@ -61,8 +61,8 @@ def tile_list_tab48_none_kernel(tc, tab, w4_words, w4_scales, tab2, u, offs, off
         nc.scalar.dma_start(rows2[96:128, :], tab2[0, 512 * T :].rearrange("(h q t) -> q h t", h=LP, t=T).bitcast(I32))
         nc.sync.dma_start(list1[:], offs)
         tab_sc = tab[:, 512 * T :].rearrange("a (q t) -> q a t", q=16).bitcast(I32)
-        nc.scalar.dma_start(rows1[96:128, :], tab_sc[:, 0:2, :])
-        nc.scalar.dma_start(rows1[80:96, :], tab_sc[:, 2, :])
+        nc.scalar.dma_start(rows1[96:128, :], tab_sc[:, 1:3, :])
+        nc.scalar.dma_start(rows1[80:96, :], tab_sc[:, 0, :])
         nc.sync.dma_start(u_raw[:].rearrange("p h j n -> p h (j n)"), u.rearrange("(h p j) n -> p h (j n)", h=LP, j=4))
         load_words(nc.sync, words2, tab2[0])
         load_words(nc.sync, words1[0], tab[0])
@@ -79,12 +79,12 @@ def tile_list_tab48_none_kernel(tc, tab, w4_words, w4_scales, tab2, u, offs, off
         words1.append(keep.tile([P, T], I32, name="words1_1", tag="turns2", align_bytes=64))
         load_words(nc.sync, words1[1], tab[1])
         nc.vector.tensor_copy(g_rows[:, 0:S], rows1[:].bitcast(U8).indirect(list1[:]))
-        for q in range(4):
-            nc.sync.dma_start(planes_tab[QUAD * q : QUAD * q + 4, :], g_rows[96 + 8 * q : 104 + 8 * q, 0:S].bitcast(I32))
+        for r in range(4):
+            nc.sync.dma_start(plane_first[r:P:QUAD, :], g_rows[80 + r : 96 : 4, 0:S].bitcast(I32))
         words1.append(keep.tile([P, T], I32, name="words1_last", tag="turns", align_bytes=64))
         load_words(nc.sync, words1[2], tab[2])
         for q in range(4):
-            nc.sync.dma_start(plane_last[QUAD * q : QUAD * q + 4, :], g_rows[80 + 4 * q : 84 + 4 * q, 0:S].bitcast(I32))
+            nc.sync.dma_start(planes_tab[QUAD * q : QUAD * q + 4, :], g_rows[96 + 8 * q : 104 + 8 * q, 0:S].bitcast(I32))
         nc.vector.tensor_copy(g_words2[:], words2[:].bitcast(U32).indirect(list2[:]))
         nc.vector.quantize_mx(
             out=u_codes[:].bitcast(FP8X4),
@@ -96,7 +96,7 @@ def tile_list_tab48_none_kernel(tc, tab, w4_words, w4_scales, tab2, u, offs, off
             parted2[:].bitcast(U16).rearrange("p (h n) -> p h n", h=LP),
             g_words2[:].bitcast(U16).rearrange("p (n h) -> p h n", h=LP),
         )
-        planes1 = [planes_tab[:].bitcast(U8)[:, S * a : S * (a + 1)] for a in range(KP - 1)] + [plane_last[:].bitcast(U8)]
+        planes1 = [plane_first[:].bitcast(U8)] + [planes_tab[:].bitcast(U8)[:, S * a : S * (a + 1)] for a in range(KP - 1)]
         planes2 = [planes_tab2[:].bitcast(U8)[:, S * h : S * (h + 1)] for h in range(LP)]
         w_sc_u8 = w_sc[:].rearrange("p a n -> p (a n)").bitcast(U8)
 

@@ -18,6 +18,7 @@ LP = L // 512
 QUAD = 32
 GROUP = 128
 GROUPS = S // GROUP
+HALF = S // 2
 FLOPS = 2 * M * S * (K + L)
 
 
@@ -40,12 +41,13 @@ def tile_list_tab48_none_kernel(tc, tab, w4_words, w4_scales, tab2, u, offs, off
         u_scales = keep.tile([P, LP * M], U8, name="u_scales", align_bytes=64)
         w_words = keep.tile([P, KP, 2 * M], U8, name="w_words", align_bytes=64)
         w_sc = keep.tile([P, KP, M // 4], I32, name="w_sc", align_bytes=64)
-        g_words2 = keep.tile([P, S], U32, name="g_words2", align_bytes=64)
+        g_words2 = [keep.tile([P, HALF], U32, name=f"g_words2_{b}", align_bytes=64) for b in range(2)]
+        parted2 = keep.tile([P, LP * 2 * S], U8, name="parted2", align_bytes=64)
         g_rows = keep.tile([P, 2 * S], U8, name="g_rows", align_bytes=64)
         planes_tab = keep.tile([P, 2 * S // 4], I32, name="planes_tab", align_bytes=64)
         planes_tab2 = keep.tile([P, 2 * S // 4], I32, name="planes_tab2", align_bytes=64)
         plane_first = keep.tile([P, S // 4], I32, name="plane_first", align_bytes=64)
-        g_words1 = [staged.tile([P, S], U32, name="g_words1_0", offset=4 * S, align_bytes=64)]
+        g_words1 = [staged.tile([P, S], U32, name="g_words1_0", offset=0, align_bytes=64)]
         g_words1 += [keep.tile([P, S], U32, name=f"g_words1_{a}", align_bytes=64) for a in range(1, KP)]
         out_a = keep.tile([P, 2 * GROUP], F32, name="out_a", align_bytes=64)
         out_b = keep.tile([P, 2 * GROUP], F32, name="out_b", align_bytes=64)
@@ -63,15 +65,18 @@ def tile_list_tab48_none_kernel(tc, tab, w4_words, w4_scales, tab2, u, offs, off
         tab_sc = tab[:, 512 * T :].rearrange("a (q t) -> q a t", q=16).bitcast(I32)
         nc.scalar.dma_start(rows1[96:128, :], tab_sc[:, 1:3, :])
         nc.scalar.dma_start(rows1[80:96, :], tab_sc[:, 0, :])
-        nc.sync.dma_start(u_raw[:].rearrange("p h j n -> p h (j n)"), u.rearrange("(h p j) n -> p h (j n)", h=LP, j=4))
         load_words(nc.sync, words2, tab2[0])
+        nc.sync.dma_start(u_raw[:].rearrange("p h j n -> p h (j n)"), u.rearrange("(h p j) n -> p h (j n)", h=LP, j=4))
         load_words(nc.sync, words1[0], tab[0])
         w_sc_src = w4_scales.rearrange("a q n -> q a n")
         for q in range(4):
             nc.gpsimd.dma_start(w_sc[QUAD * q : QUAD * q + 4, :, :], w_sc_src[4 * q : 4 * q + 4].bitcast(I32))
         nc.gpsimd.dma_start(w_words[:].bitcast(I32), w4_words.rearrange("a p b -> p a b").bitcast(I32))
 
-        nc.scalar.copy(u_bf[:], u_raw[:].rearrange("p h j n -> p h n j"))
+        nc.scalar.copy(
+            u_bf[:].rearrange("p h (c i) j -> p h c j i", i=4),
+            u_raw[:].rearrange("p h j (c i) -> p h c j i", i=4),
+        )
 
         nc.vector.tensor_copy(g_rows[:, S : 2 * S], rows2[:].bitcast(U8).indirect(list2[:]))
         for q in range(4):
@@ -85,16 +90,18 @@ def tile_list_tab48_none_kernel(tc, tab, w4_words, w4_scales, tab2, u, offs, off
         load_words(nc.sync, words1[2], tab[2])
         for q in range(4):
             nc.sync.dma_start(planes_tab[QUAD * q : QUAD * q + 4, :], g_rows[96 + 8 * q : 104 + 8 * q, 0:S].bitcast(I32))
-        nc.vector.tensor_copy(g_words2[:], words2[:].bitcast(U32).indirect(list2[:]))
+        halves = [slice(HALF * b, HALF * (b + 1)) for b in range(2)]
+        for b, cols in enumerate(halves):
+            nc.vector.tensor_copy(g_words2[b][:], words2[:].bitcast(U32).indirect(list2[:, cols.start // 16 : cols.stop // 16]))
+        for b, cols in enumerate(halves):
+            nc.vector.tensor_copy(
+                parted2[:].bitcast(U16).rearrange("p (h n) -> p h n", h=LP)[:, :, cols],
+                g_words2[b][:].bitcast(U16).rearrange("p (n h) -> p h n", h=LP),
+            )
         nc.vector.quantize_mx(
             out=u_codes[:].bitcast(FP8X4),
             scales=u_scales[:],
             in_=u_bf[:].rearrange("p h n j -> p (h n j)"),
-        )
-        parted2 = staged.tile([P, LP * 2 * S], U8, name="parted2", offset=0, align_bytes=64)
-        nc.vector.tensor_copy(
-            parted2[:].bitcast(U16).rearrange("p (h n) -> p h n", h=LP),
-            g_words2[:].bitcast(U16).rearrange("p (n h) -> p h n", h=LP),
         )
         planes1 = [plane_first[:].bitcast(U8)] + [planes_tab[:].bitcast(U8)[:, S * a : S * (a + 1)] for a in range(KP - 1)]
         planes2 = [planes_tab2[:].bitcast(U8)[:, S * h : S * (h + 1)] for h in range(LP)]

@@ -53,8 +53,9 @@ def tile_list_tab48_none_kernel(tc, tab, w4_words, w4_scales, tab2, u, offs, off
         out_b = keep.tile([P, 2 * GROUP], F32, name="out_b", align_bytes=64)
         banks = [psum.tile([P, 512], F32, name=f"bank{g}") for g in range(GROUPS)]
 
-        nc.vector.memset(rows2[0:96, :], 0)
-        nc.vector.memset(rows1[0:80, :], 0)
+        for rows, top in ((rows2, 96), (rows1, 80)):
+            nc.vector.memset(rows[0:top, 0 : T // 4 - 1], 0)
+            nc.vector.memset(rows[0:top, T // 4 - 1 : T // 4], 0)
 
         def load_words(eng, tile, src):
             eng.dma_start(tile[:], src[0 : 512 * T].rearrange("(p b) -> p b", p=P).bitcast(I32))
@@ -71,7 +72,8 @@ def tile_list_tab48_none_kernel(tc, tab, w4_words, w4_scales, tab2, u, offs, off
         w_sc_src = w4_scales.rearrange("a q n -> q a n")
         for q in range(4):
             nc.gpsimd.dma_start(w_sc[QUAD * q : QUAD * q + 4, :, :], w_sc_src[4 * q : 4 * q + 4].bitcast(I32))
-        nc.gpsimd.dma_start(w_words[:].bitcast(I32), w4_words.rearrange("a p b -> p a b").bitcast(I32))
+            if q == 0:
+                nc.gpsimd.dma_start(w_words[:].bitcast(I32), w4_words.rearrange("a p b -> p a b").bitcast(I32))
 
         nc.scalar.copy(
             u_bf[:].rearrange("p h (c i) j -> p h c j i", i=4),

@@ -49,8 +49,8 @@ def tile_list_tab48_none_kernel(tc, tab, w4_words, w4_scales, tab2, u, offs, off
         plane_first = keep.tile([P, S // 4], I32, name="plane_first", align_bytes=64)
         g_words1 = [staged.tile([P, S], U32, name="g_words1_0", offset=0, align_bytes=64)]
         g_words1 += [keep.tile([P, S], U32, name=f"g_words1_{a}", align_bytes=64) for a in range(1, KP)]
-        out_a = keep.tile([P, 2 * GROUP], F32, name="out_a", align_bytes=64)
-        out_b = keep.tile([P, 2 * GROUP], F32, name="out_b", align_bytes=64)
+        out_0 = keep.tile([P, 2 * GROUP], F32, name="out_0", align_bytes=64)
+        out_1 = keep.tile([P, 2 * GROUP], F32, name="out_1", align_bytes=64)
         banks = [psum.tile([P, 512], F32, name=f"bank{g}") for g in range(GROUPS)]
 
         for rows, top in ((rows2, 96), (rows1, 80)):
@@ -72,7 +72,7 @@ def tile_list_tab48_none_kernel(tc, tab, w4_words, w4_scales, tab2, u, offs, off
         w_sc_src = w4_scales.rearrange("a q n -> q a n")
         for q in range(4):
             nc.gpsimd.dma_start(w_sc[QUAD * q : QUAD * q + 4, :, :], w_sc_src[4 * q : 4 * q + 4].bitcast(I32))
-            if q == 0:
+            if q == 2:
                 nc.gpsimd.dma_start(w_words[:].bitcast(I32), w4_words.rearrange("a p b -> p a b").bitcast(I32))
 
         nc.scalar.copy(
@@ -145,10 +145,10 @@ def tile_list_tab48_none_kernel(tc, tab, w4_words, w4_scales, tab2, u, offs, off
         multiply2(1)
         gather_and_multiply(0, (S,))
         gather_and_multiply(1, (S,))
-        gather_and_multiply(2, (2 * GROUP, GROUP, GROUP))
-        for g in range(2):
-            nc.scalar.copy(out_a[:, GROUP * g : GROUP * (g + 1)], banks[g][:, 0:GROUP])
-        nc.sync.dma_start(out[:, 0 : 2 * GROUP], out_a[:])
-        nc.scalar.copy(out_b[:, 0:GROUP], banks[2][:, 0:GROUP])
-        nc.vector.tensor_copy(out_b[:, GROUP : 2 * GROUP], banks[3][:, 0:GROUP])
-        nc.scalar.dma_start(out[:, 2 * GROUP : S], out_b[:])
+        gather_and_multiply(2, (2 * GROUP, GROUP, GROUP,))
+        nc.scalar.copy(out_0[:, 0 * GROUP : 1 * GROUP], banks[0][:, 0:GROUP])
+        nc.scalar.copy(out_0[:, 1 * GROUP : 2 * GROUP], banks[1][:, 0:GROUP])
+        nc.sync.dma_start(out[:, 0 * GROUP : 2 * GROUP], out_0[:])
+        nc.vector.tensor_copy(out_1[:, 0 * GROUP : 1 * GROUP], banks[2][:, 0:GROUP])
+        nc.scalar.copy(out_1[:, 1 * GROUP : 2 * GROUP], banks[3][:, 0:GROUP])
+        nc.scalar.dma_start(out[:, 2 * GROUP : 4 * GROUP], out_1[:])

@@ -13,12 +13,19 @@ FP4X4 = mybir.dt.float4_e2m1fn_x4
 
 P = 128
 K, L, M, T, S = 1536, 1024, 128, 1024, 512
-KP = K // 512
-LP = L // 512
+PASS = 512
+KP = K // PASS
+LP = L // PASS
+BLOCKS = PASS // 32
 QUAD = 32
+LIVE = 4
+PER_COLUMN = 16
+WORD_BYTES = 4 * P * T
 GROUP = 128
 GROUPS = S // GROUP
 HALF = S // 2
+PAIR_ROWS = P - 2 * BLOCKS
+FIRST_ROWS = PAIR_ROWS - BLOCKS
 FLOPS = 2 * M * S * (K + L)
 
 
@@ -29,10 +36,10 @@ def tile_list_tab48_none_kernel(tc, tab, w4_words, w4_scales, tab2, u, offs, off
         staged = ctx.enter_context(tc.tile_pool(name="staged", bufs=1))
         psum = ctx.enter_context(tc.psum_pool(name="psum", bufs=1))
 
-        list1 = keep.tile([P, S // 16], U16, name="list1")
-        list2 = keep.tile([P, S // 16], U16, name="list2")
-        rows1 = keep.tile([P, T // 4], I32, name="rows1", tag="turns", align_bytes=64)
-        rows2 = keep.tile([P, T // 4], I32, name="rows2", tag="turns2", align_bytes=64)
+        list1 = keep.tile([P, S // PER_COLUMN], U16, name="list1")
+        list2 = keep.tile([P, S // PER_COLUMN], U16, name="list2")
+        rows1 = keep.tile([P, T // 4], I32, name="rows1", tag="after_rows1", align_bytes=64)
+        rows2 = keep.tile([P, T // 4], I32, name="rows2", tag="after_rows2", align_bytes=64)
         words2 = keep.tile([P, T], I32, name="words2", align_bytes=64)
         words1 = [keep.tile([P, T], I32, name="words1_0", align_bytes=64)]
         u_raw = staged.tile([P, LP, 4, M], F32, name="u_raw", offset=0, align_bytes=64)
@@ -40,100 +47,112 @@ def tile_list_tab48_none_kernel(tc, tab, w4_words, w4_scales, tab2, u, offs, off
         u_codes = keep.tile([P, LP * M], U32, name="u_codes", align_bytes=64)
         u_scales = keep.tile([P, LP * M], U8, name="u_scales", align_bytes=64)
         w_words = keep.tile([P, KP, 2 * M], U8, name="w_words", align_bytes=64)
-        w_sc = keep.tile([P, KP, M // 4], I32, name="w_sc", align_bytes=64)
-        g_words2 = [keep.tile([P, HALF], U32, name=f"g_words2_{b}", align_bytes=64) for b in range(2)]
-        parted2 = keep.tile([P, LP * 2 * S], U8, name="parted2", align_bytes=64)
+        w_planes = keep.tile([P, KP, M // 4], I32, name="w_planes", align_bytes=64)
+        g_words2 = keep.tile([P, S], U32, name="g_words2", align_bytes=64)
+        parted2 = [
+            staged.tile([P, LP * 2 * HALF], U8, name=f"parted2_{b}", offset=LP * 2 * HALF * b, align_bytes=64)
+            for b in range(2)
+        ]
         g_rows = keep.tile([P, 2 * S], U8, name="g_rows", align_bytes=64)
         planes_tab = keep.tile([P, 2 * S // 4], I32, name="planes_tab", align_bytes=64)
         planes_tab2 = keep.tile([P, 2 * S // 4], I32, name="planes_tab2", align_bytes=64)
         plane_first = keep.tile([P, S // 4], I32, name="plane_first", align_bytes=64)
-        g_words1 = [staged.tile([P, S], U32, name="g_words1_0", offset=0, align_bytes=64)]
+        g_words1 = [staged.tile([P, S], U32, name="g_words1_0", offset=LP * 2 * S, align_bytes=64)]
         g_words1 += [keep.tile([P, S], U32, name=f"g_words1_{a}", align_bytes=64) for a in range(1, KP)]
-        out_0 = keep.tile([P, 2 * GROUP], F32, name="out_0", align_bytes=64)
-        out_1 = keep.tile([P, 2 * GROUP], F32, name="out_1", align_bytes=64)
+        out_0 = keep.tile([P, HALF], F32, name="out_0", align_bytes=64)
+        out_1 = keep.tile([P, HALF], F32, name="out_1", align_bytes=64)
         banks = [psum.tile([P, 512], F32, name=f"bank{g}") for g in range(GROUPS)]
 
-        for rows, top in ((rows2, 96), (rows1, 80)):
+        for rows, top in ((rows2, PAIR_ROWS), (rows1, FIRST_ROWS)):
             nc.vector.memset(rows[0:top, 0 : T // 4 - 1], 0)
             nc.vector.memset(rows[0:top, T // 4 - 1 : T // 4], 0)
 
-        def load_words(eng, tile, src):
-            eng.dma_start(tile[:], src[0 : 512 * T].rearrange("(p b) -> p b", p=P).bitcast(I32))
+        def load_words(tile, table_row):
+            nc.sync.dma_start(tile[:], table_row[0:WORD_BYTES].rearrange("(p b) -> p b", p=P).bitcast(I32))
 
         nc.sync.dma_start(list2[:], offs2)
-        nc.scalar.dma_start(rows2[96:128, :], tab2[0, 512 * T :].rearrange("(h q t) -> q h t", h=LP, t=T).bitcast(I32))
+        nc.scalar.dma_start(rows2[PAIR_ROWS:P, :], tab2[0, WORD_BYTES:].rearrange("(h q t) -> q h t", h=LP, t=T).bitcast(I32))
         nc.sync.dma_start(list1[:], offs)
-        tab_sc = tab[:, 512 * T :].rearrange("a (q t) -> q a t", q=16).bitcast(I32)
-        nc.scalar.dma_start(rows1[96:128, :], tab_sc[:, 1:3, :])
-        nc.scalar.dma_start(rows1[80:96, :], tab_sc[:, 0, :])
-        load_words(nc.sync, words2, tab2[0])
-        nc.sync.dma_start(u_raw[:].rearrange("p h j n -> p h (j n)"), u.rearrange("(h p j) n -> p h (j n)", h=LP, j=4))
-        load_words(nc.sync, words1[0], tab[0])
-        w_sc_src = w4_scales.rearrange("a q n -> q a n")
-        for q in range(4):
-            nc.gpsimd.dma_start(w_sc[QUAD * q : QUAD * q + 4, :, :], w_sc_src[4 * q : 4 * q + 4].bitcast(I32))
-            if q == 2:
-                nc.gpsimd.dma_start(w_words[:].bitcast(I32), w4_words.rearrange("a p b -> p a b").bitcast(I32))
+        tab_rows = tab[:, WORD_BYTES:].rearrange("a (q t) -> q a t", q=BLOCKS).bitcast(I32)
+        nc.scalar.dma_start(rows1[PAIR_ROWS:P, :], tab_rows[:, 1:KP, :])
+        nc.scalar.dma_start(rows1[FIRST_ROWS:PAIR_ROWS, :], tab_rows[:, 0, :])
+        nc.sync.dma_start(u_raw[:].rearrange("p h i n -> p h (i n)"), u.rearrange("(h p i) n -> p h (i n)", h=LP, i=4))
+        load_words(words2, tab2[0])
+        load_words(words1[0], tab[0])
+
+        w_rows = w4_scales.rearrange("a q n -> q a n")
+
+        def load_w_planes(quad):
+            nc.gpsimd.dma_start(w_planes[QUAD * quad : QUAD * quad + LIVE, :, :], w_rows[LIVE * quad : LIVE * (quad + 1)].bitcast(I32))
+
+        last_quad = P // QUAD - 1
+        for quad in range(last_quad):
+            load_w_planes(quad)
+        nc.gpsimd.dma_start(w_words[:].bitcast(I32), w4_words.rearrange("a p b -> p a b").bitcast(I32))
+        load_w_planes(last_quad)
 
         nc.scalar.copy(
-            u_bf[:].rearrange("p h (c i) j -> p h c j i", i=4),
-            u_raw[:].rearrange("p h j (c i) -> p h c j i", i=4),
+            u_bf[:].rearrange("p h (c e) i -> p h c i e", e=4),
+            u_raw[:].rearrange("p h i (c e) -> p h c i e", e=4),
         )
 
+        def carry_pair(planes, cols):
+            for quad in range(P // QUAD):
+                first = PAIR_ROWS + 2 * LIVE * quad
+                nc.sync.dma_start(planes[QUAD * quad : QUAD * quad + LIVE, :], g_rows[first : first + 2 * LIVE, cols].bitcast(I32))
+
         nc.vector.tensor_copy(g_rows[:, S : 2 * S], rows2[:].bitcast(U8).indirect(list2[:]))
-        for q in range(4):
-            nc.sync.dma_start(planes_tab2[QUAD * q : QUAD * q + 4, :], g_rows[96 + 8 * q : 104 + 8 * q, S : 2 * S].bitcast(I32))
-        words1.append(keep.tile([P, T], I32, name="words1_1", tag="turns2", align_bytes=64))
-        load_words(nc.sync, words1[1], tab[1])
+        carry_pair(planes_tab2, slice(S, 2 * S))
+        words1.append(keep.tile([P, T], I32, name="words1_1", tag="after_rows2", align_bytes=64))
+        load_words(words1[1], tab[1])
         nc.vector.tensor_copy(g_rows[:, 0:S], rows1[:].bitcast(U8).indirect(list1[:]))
-        for r in range(4):
-            nc.sync.dma_start(plane_first[r:P:QUAD, :], g_rows[80 + r : 96 : 4, 0:S].bitcast(I32))
-        words1.append(keep.tile([P, T], I32, name="words1_last", tag="turns", align_bytes=64))
-        load_words(nc.sync, words1[2], tab[2])
-        for q in range(4):
-            nc.sync.dma_start(planes_tab[QUAD * q : QUAD * q + 4, :], g_rows[96 + 8 * q : 104 + 8 * q, 0:S].bitcast(I32))
-        halves = [slice(HALF * b, HALF * (b + 1)) for b in range(2)]
-        for b, cols in enumerate(halves):
-            nc.vector.tensor_copy(g_words2[b][:], words2[:].bitcast(U32).indirect(list2[:, cols.start // 16 : cols.stop // 16]))
-        for b, cols in enumerate(halves):
-            nc.vector.tensor_copy(
-                parted2[:].bitcast(U16).rearrange("p (h n) -> p h n", h=LP)[:, :, cols],
-                g_words2[b][:].bitcast(U16).rearrange("p (n h) -> p h n", h=LP),
-            )
+        for r in range(LIVE):
+            nc.sync.dma_start(plane_first[r:P:QUAD, :], g_rows[FIRST_ROWS + r : PAIR_ROWS : LIVE, 0:S].bitcast(I32))
+        words1.append(keep.tile([P, T], I32, name="words1_2", tag="after_rows1", align_bytes=64))
+        load_words(words1[2], tab[2])
+        carry_pair(planes_tab, slice(0, S))
+
+        nc.vector.tensor_copy(g_words2[:], words2[:].bitcast(U32).indirect(list2[:]))
         nc.vector.quantize_mx(
             out=u_codes[:].bitcast(FP8X4),
             scales=u_scales[:],
-            in_=u_bf[:].rearrange("p h n j -> p (h n j)"),
+            in_=u_bf[:].rearrange("p h n i -> p (h n i)"),
         )
-        planes1 = [plane_first[:].bitcast(U8)] + [planes_tab[:].bitcast(U8)[:, S * a : S * (a + 1)] for a in range(KP - 1)]
-        planes2 = [planes_tab2[:].bitcast(U8)[:, S * h : S * (h + 1)] for h in range(LP)]
-        w_sc_u8 = w_sc[:].rearrange("p a n -> p (a n)").bitcast(U8)
+        for b in range(2):
+            nc.vector.tensor_copy(
+                parted2[b][:].bitcast(U16).rearrange("p (h n) -> p h n", h=LP),
+                g_words2[:, HALF * b : HALF * (b + 1)].bitcast(U16).rearrange("p (n h) -> p h n", h=LP),
+            )
 
-        def multiply2(h):
-            plane = planes2[h]
-            for g in range(GROUPS):
-                nc.tensor.matmul_mx(
-                    out=banks[g][:, 0:GROUP],
-                    lhsT=u_codes[:, M * h : M * (h + 1)].bitcast(FP8X4),
-                    lhsT_scale=u_scales[:, M * h : M * (h + 1)],
-                    rhs=parted2[:, 2 * S * h + 2 * GROUP * g : 2 * S * h + 2 * GROUP * (g + 1)].bitcast(FP4X4),
-                    rhs_scale=plane[:, GROUP * g : GROUP * (g + 1)],
-                    start=(h == 0),
-                    stop=False,
-                )
+        planes1 = [plane_first[:].bitcast(U8)] + [planes_tab[:].bitcast(U8)[:, S * s : S * (s + 1)] for s in range(KP - 1)]
+        planes2 = [planes_tab2[:].bitcast(U8)[:, S * h : S * (h + 1)] for h in range(LP)]
+        w_planes_u8 = w_planes[:].rearrange("p a n -> p (a n)").bitcast(U8)
+
+        for b in range(2):
+            for h in range(LP):
+                for c in range(HALF // GROUP):
+                    g = b * (HALF // GROUP) + c
+                    first = 2 * (HALF * h + GROUP * c)
+                    nc.tensor.matmul_mx(
+                        out=banks[g][:, 0:GROUP],
+                        lhsT=u_codes[:, M * h : M * (h + 1)].bitcast(FP8X4),
+                        lhsT_scale=u_scales[:, M * h : M * (h + 1)],
+                        rhs=parted2[b][:, first : first + 2 * GROUP].bitcast(FP4X4),
+                        rhs_scale=planes2[h][:, GROUP * g : GROUP * (g + 1)],
+                        start=(h == 0),
+                        stop=False,
+                    )
 
         def gather_and_multiply(a, pieces):
             done = 0
             for piece in pieces:
-                nc.vector.tensor_copy(
-                    g_words1[a][:, done : done + piece],
-                    words1[a][:].bitcast(U32).indirect(list1[:, done // 16 : (done + piece) // 16]),
-                )
+                entries = list1[:, done // PER_COLUMN : (done + piece) // PER_COLUMN]
+                nc.vector.tensor_copy(g_words1[a][:, done : done + piece], words1[a][:].bitcast(U32).indirect(entries))
                 for g in range(done // GROUP, (done + piece) // GROUP):
                     nc.tensor.matmul_mx(
                         out=banks[g][:, 0:GROUP],
                         lhsT=w_words[:, a, :].bitcast(FP4X4),
-                        lhsT_scale=w_sc_u8[:, M * a : M * (a + 1)],
+                        lhsT_scale=w_planes_u8[:, M * a : M * (a + 1)],
                         rhs=g_words1[a][:, GROUP * g : GROUP * (g + 1)].bitcast(FP8X4),
                         rhs_scale=planes1[a][:, GROUP * g : GROUP * (g + 1)],
                         start=False,
@@ -141,14 +160,13 @@ def tile_list_tab48_none_kernel(tc, tab, w4_words, w4_scales, tab2, u, offs, off
                     )
                 done += piece
 
-        multiply2(0)
-        multiply2(1)
-        gather_and_multiply(0, (S,))
-        gather_and_multiply(1, (S,))
-        gather_and_multiply(2, (2 * GROUP, GROUP, GROUP,))
-        nc.scalar.copy(out_0[:, 0 * GROUP : 1 * GROUP], banks[0][:, 0:GROUP])
-        nc.scalar.copy(out_0[:, 1 * GROUP : 2 * GROUP], banks[1][:, 0:GROUP])
-        nc.sync.dma_start(out[:, 0 * GROUP : 2 * GROUP], out_0[:])
-        nc.vector.tensor_copy(out_1[:, 0 * GROUP : 1 * GROUP], banks[2][:, 0:GROUP])
-        nc.scalar.copy(out_1[:, 1 * GROUP : 2 * GROUP], banks[3][:, 0:GROUP])
-        nc.scalar.dma_start(out[:, 2 * GROUP : 4 * GROUP], out_1[:])
+        for a in range(KP - 1):
+            gather_and_multiply(a, (S,))
+        gather_and_multiply(KP - 1, (HALF, GROUP, GROUP))
+
+        nc.scalar.copy(out_0[:, 0:GROUP], banks[0][:, 0:GROUP])
+        nc.scalar.copy(out_0[:, GROUP:HALF], banks[1][:, 0:GROUP])
+        nc.sync.dma_start(out[:, 0:HALF], out_0[:])
+        nc.vector.tensor_copy(out_1[:, 0:GROUP], banks[2][:, 0:GROUP])
+        nc.scalar.copy(out_1[:, GROUP:HALF], banks[3][:, 0:GROUP])
+        nc.scalar.dma_start(out[:, HALF:S], out_1[:])

@@ -120,8 +120,8 @@ def tile_list_tab48_none_kernel(tc, tab, w4_words, w4_scales, tab2, u, offs, off
         )
         for b in range(2):
             nc.vector.tensor_copy(
-                parted2[b][:].bitcast(U16).rearrange("p (h n) -> p h n", h=LP),
-                g_words2[:, HALF * b : HALF * (b + 1)].bitcast(U16).rearrange("p (n h) -> p h n", h=LP),
+                parted2[b][:].bitcast(U16).rearrange("p (h c n) -> p c h n", h=LP, n=GROUP),
+                g_words2[:, HALF * b : HALF * (b + 1)].bitcast(U16).rearrange("p (c n h) -> p c h n", h=LP, n=GROUP),
             )
 
         planes1 = [plane_first[:].bitcast(U8)] + [planes_tab[:].bitcast(U8)[:, S * s : S * (s + 1)] for s in range(KP - 1)]

@@ -49,15 +49,12 @@ def tile_list_tab48_none_kernel(tc, tab, w4_words, w4_scales, tab2, u, offs, off
         w_words = keep.tile([P, KP, 2 * M], U8, name="w_words", align_bytes=64)
         w_planes = keep.tile([P, KP, M // 4], I32, name="w_planes", align_bytes=64)
         g_words2 = keep.tile([P, S], U32, name="g_words2", align_bytes=64)
-        parted2 = [
-            staged.tile([P, LP * 2 * HALF], U8, name=f"parted2_{b}", offset=LP * 2 * HALF * b, align_bytes=64)
-            for b in range(2)
-        ]
+        parted2 = [keep.tile([P, LP * 2 * HALF], U8, name=f"parted2_{b}", align_bytes=64) for b in range(2)]
         g_rows = keep.tile([P, 2 * S], U8, name="g_rows", align_bytes=64)
         planes_tab = keep.tile([P, 2 * S // 4], I32, name="planes_tab", align_bytes=64)
         planes_tab2 = keep.tile([P, 2 * S // 4], I32, name="planes_tab2", align_bytes=64)
         plane_first = keep.tile([P, S // 4], I32, name="plane_first", align_bytes=64)
-        g_words1 = [staged.tile([P, S], U32, name="g_words1_0", offset=LP * 2 * S, align_bytes=64)]
+        g_words1 = [staged.tile([P, S], U32, name="g_words1_0", offset=0, align_bytes=64)]
         g_words1 += [keep.tile([P, S], U32, name=f"g_words1_{a}", align_bytes=64) for a in range(1, KP)]
         out_0 = keep.tile([P, HALF], F32, name="out_0", align_bytes=64)
         out_1 = keep.tile([P, HALF], F32, name="out_1", align_bytes=64)
@@ -75,9 +72,9 @@ def tile_list_tab48_none_kernel(tc, tab, w4_words, w4_scales, tab2, u, offs, off
         nc.sync.dma_start(list1[:], offs)
         tab_rows = tab[:, WORD_BYTES:].rearrange("a (q t) -> q a t", q=BLOCKS).bitcast(I32)
         nc.scalar.dma_start(rows1[PAIR_ROWS:P, :], tab_rows[:, 1:KP, :])
-        nc.scalar.dma_start(rows1[FIRST_ROWS:PAIR_ROWS, :], tab_rows[:, 0, :])
-        nc.sync.dma_start(u_raw[:].rearrange("p h i n -> p h (i n)"), u.rearrange("(h p i) n -> p h (i n)", h=LP, i=4))
+        nc.sync.dma_start(rows1[FIRST_ROWS:PAIR_ROWS, :], tab_rows[:, 0, :])
         load_words(words2, tab2[0])
+        nc.sync.dma_start(u_raw[:].rearrange("p h i n -> p h (i n)"), u.rearrange("(h p i) n -> p h (i n)", h=LP, i=4))
         load_words(words1[0], tab[0])
 
         w_rows = w4_scales.rearrange("a q n -> q a n")
@@ -112,17 +109,20 @@ def tile_list_tab48_none_kernel(tc, tab, w4_words, w4_scales, tab2, u, offs, off
         load_words(words1[2], tab[2])
         carry_pair(planes_tab, slice(0, S))
 
-        nc.vector.tensor_copy(g_words2[:], words2[:].bitcast(U32).indirect(list2[:]))
-        nc.vector.quantize_mx(
-            out=u_codes[:].bitcast(FP8X4),
-            scales=u_scales[:],
-            in_=u_bf[:].rearrange("p h n i -> p (h n i)"),
-        )
+        for b in range(2):
+            entries = list2[:, HALF * b // PER_COLUMN : HALF * (b + 1) // PER_COLUMN]
+            nc.vector.tensor_copy(g_words2[:, HALF * b : HALF * (b + 1)], words2[:].bitcast(U32).indirect(entries))
         for b in range(2):
             nc.vector.tensor_copy(
                 parted2[b][:].bitcast(U16).rearrange("p (h c n) -> p c h n", h=LP, n=GROUP),
                 g_words2[:, HALF * b : HALF * (b + 1)].bitcast(U16).rearrange("p (c n h) -> p c h n", h=LP, n=GROUP),
             )
+
+        nc.vector.quantize_mx(
+            out=u_codes[:].bitcast(FP8X4),
+            scales=u_scales[:],
+            in_=u_bf[:].rearrange("p h n i -> p (h n i)"),
+        )
 
         planes1 = [plane_first[:].bitcast(U8)] + [planes_tab[:].bitcast(U8)[:, S * s : S * (s + 1)] for s in range(KP - 1)]
         planes2 = [planes_tab2[:].bitcast(U8)[:, S * h : S * (h + 1)] for h in range(LP)]

@@ -72,7 +72,7 @@ def tile_list_tab48_none_kernel(tc, tab, w4_words, w4_scales, tab2, u, offs, off
         nc.sync.dma_start(list1[:], offs)
         tab_rows = tab[:, WORD_BYTES:].rearrange("a (q t) -> q a t", q=BLOCKS).bitcast(I32)
         nc.scalar.dma_start(rows1[PAIR_ROWS:P, :], tab_rows[:, 1:KP, :])
-        nc.sync.dma_start(rows1[FIRST_ROWS:PAIR_ROWS, :], tab_rows[:, 0, :])
+        nc.scalar.dma_start(rows1[FIRST_ROWS:PAIR_ROWS, :], tab_rows[:, 0, :])
         load_words(words2, tab2[0])
         nc.sync.dma_start(u_raw[:].rearrange("p h i n -> p h (i n)"), u.rearrange("(h p i) n -> p h (i n)", h=LP, i=4))
         load_words(words1[0], tab[0])

@@ -67,8 +67,8 @@ def tile_list_tab48_none_kernel(tc, tab, w4_words, w4_scales, tab2, u, offs, off
         def load_words(tile, table_row):
             nc.sync.dma_start(tile[:], table_row[0:WORD_BYTES].rearrange("(p b) -> p b", p=P).bitcast(I32))
 
-        nc.sync.dma_start(list2[:], offs2)
         nc.scalar.dma_start(rows2[PAIR_ROWS:P, :], tab2[0, WORD_BYTES:].rearrange("(h q t) -> q h t", h=LP, t=T).bitcast(I32))
+        nc.sync.dma_start(list2[:], offs2)
         nc.sync.dma_start(list1[:], offs)
         tab_rows = tab[:, WORD_BYTES:].rearrange("a (q t) -> q a t", q=BLOCKS).bitcast(I32)
         nc.scalar.dma_start(rows1[PAIR_ROWS:P, :], tab_rows[:, 1:KP, :])

from contextlib import ExitStack

import concourse.mybir as mybir

F32 = mybir.dt.float32
BF16 = mybir.dt.bfloat16
I32 = mybir.dt.int32
U32 = mybir.dt.uint32
U16 = mybir.dt.uint16
U8 = mybir.dt.uint8
FP8X4 = mybir.dt.float8_e4m3fn_x4
FP4X4 = mybir.dt.float4_e2m1fn_x4

P = 128
K, L, M, T, S = 1536, 1024, 128, 1024, 512
PASS = 512
KP = K // PASS
LP = L // PASS
BLOCKS = PASS // 32
QUAD = 32
LIVE = 4
PER_COLUMN = 16
WORD_BYTES = 4 * P * T
GROUP = 128
GROUPS = S // GROUP
HALF = S // 2
PAIR_ROWS = P - 2 * BLOCKS
FIRST_ROWS = PAIR_ROWS - BLOCKS
FLOPS = 2 * M * S * (K + L)


def tile_list_tab48_none_kernel(tc, tab, w4_words, w4_scales, tab2, u, offs, offs2, out):
    nc = tc.nc
    with ExitStack() as ctx:
        keep = ctx.enter_context(tc.tile_pool(name="keep", bufs=1))
        staged = ctx.enter_context(tc.tile_pool(name="staged", bufs=1))
        psum = ctx.enter_context(tc.psum_pool(name="psum", bufs=1))

        list1 = keep.tile([P, S // PER_COLUMN], U16, name="list1")
        list2 = keep.tile([P, S // PER_COLUMN], U16, name="list2")
        rows1 = keep.tile([P, T // 4], I32, name="rows1", tag="after_rows1", align_bytes=64)
        rows2 = keep.tile([P, T // 4], I32, name="rows2", tag="after_rows2", align_bytes=64)
        words2 = keep.tile([P, T], I32, name="words2", align_bytes=64)
        words1 = [keep.tile([P, T], I32, name="words1_0", align_bytes=64)]
        u_raw = staged.tile([P, LP, 4, M], F32, name="u_raw", offset=0, align_bytes=64)
        u_bf = keep.tile([P, LP, M, 4], BF16, name="u_bf", align_bytes=64)
        u_codes = keep.tile([P, LP * M], U32, name="u_codes", align_bytes=64)
        u_scales = keep.tile([P, LP * M], U8, name="u_scales", align_bytes=64)
        w_words = keep.tile([P, KP, 2 * M], U8, name="w_words", align_bytes=64)
        w_planes = keep.tile([P, KP, M // 4], I32, name="w_planes", align_bytes=64)
        g_words2 = keep.tile([P, S], U32, name="g_words2", align_bytes=64)
        parted2 = [keep.tile([P, LP * 2 * HALF], U8, name=f"parted2_{b}", align_bytes=64) for b in range(2)]
        g_rows = keep.tile([P, 2 * S], U8, name="g_rows", align_bytes=64)
        planes_tab = keep.tile([P, 2 * S // 4], I32, name="planes_tab", align_bytes=64)
        planes_tab2 = keep.tile([P, 2 * S // 4], I32, name="planes_tab2", align_bytes=64)
        plane_first = keep.tile([P, S // 4], I32, name="plane_first", align_bytes=64)
        g_words1 = [staged.tile([P, S], U32, name="g_words1_0", offset=0, align_bytes=64)]
        g_words1 += [keep.tile([P, S], U32, name=f"g_words1_{a}", align_bytes=64) for a in range(1, KP)]
        out_0 = keep.tile([P, HALF], F32, name="out_0", align_bytes=64)
        out_1 = keep.tile([P, HALF], F32, name="out_1", align_bytes=64)
        banks = [psum.tile([P, 512], F32, name=f"bank{g}") for g in range(GROUPS)]

        for rows, top in ((rows2, PAIR_ROWS), (rows1, FIRST_ROWS)):
            nc.vector.memset(rows[0:top, 0 : T // 4 - 1], 0)
            nc.vector.memset(rows[0:top, T // 4 - 1 : T // 4], 0)

        def load_words(tile, table_row):
            nc.sync.dma_start(tile[:], table_row[0:WORD_BYTES].rearrange("(p b) -> p b", p=P).bitcast(I32))

        nc.scalar.dma_start(rows2[PAIR_ROWS:P, :], tab2[0, WORD_BYTES:].rearrange("(h q t) -> q h t", h=LP, t=T).bitcast(I32))
        nc.sync.dma_start(list2[:], offs2)
        nc.sync.dma_start(list1[:], offs)
        tab_rows = tab[:, WORD_BYTES:].rearrange("a (q t) -> q a t", q=BLOCKS).bitcast(I32)
        nc.scalar.dma_start(rows1[PAIR_ROWS:P, :], tab_rows[:, 1:KP, :])
        nc.scalar.dma_start(rows1[FIRST_ROWS:PAIR_ROWS, :], tab_rows[:, 0, :])
        load_words(words2, tab2[0])
        nc.sync.dma_start(u_raw[:].rearrange("p h i n -> p h (i n)"), u.rearrange("(h p i) n -> p h (i n)", h=LP, i=4))
        load_words(words1[0], tab[0])

        w_rows = w4_scales.rearrange("a q n -> q a n")

        def load_w_planes(quad):
            nc.gpsimd.dma_start(w_planes[QUAD * quad : QUAD * quad + LIVE, :, :], w_rows[LIVE * quad : LIVE * (quad + 1)].bitcast(I32))

        last_quad = P // QUAD - 1
        for quad in range(last_quad):
            load_w_planes(quad)
        nc.gpsimd.dma_start(w_words[:].bitcast(I32), w4_words.rearrange("a p b -> p a b").bitcast(I32))
        load_w_planes(last_quad)

        nc.scalar.copy(
            u_bf[:].rearrange("p h (c e) i -> p h c i e", e=4),
            u_raw[:].rearrange("p h i (c e) -> p h c i e", e=4),
        )

        def carry_pair(planes, cols):
            for quad in range(P // QUAD):
                first = PAIR_ROWS + 2 * LIVE * quad
                nc.sync.dma_start(planes[QUAD * quad : QUAD * quad + LIVE, :], g_rows[first : first + 2 * LIVE, cols].bitcast(I32))

        nc.vector.tensor_copy(g_rows[:, S : 2 * S], rows2[:].bitcast(U8).indirect(list2[:]))
        carry_pair(planes_tab2, slice(S, 2 * S))
        words1.append(keep.tile([P, T], I32, name="words1_1", tag="after_rows2", align_bytes=64))
        load_words(words1[1], tab[1])
        nc.vector.tensor_copy(g_rows[:, 0:S], rows1[:].bitcast(U8).indirect(list1[:]))
        for r in range(LIVE):
            nc.sync.dma_start(plane_first[r:P:QUAD, :], g_rows[FIRST_ROWS + r : PAIR_ROWS : LIVE, 0:S].bitcast(I32))
        words1.append(keep.tile([P, T], I32, name="words1_2", tag="after_rows1", align_bytes=64))
        load_words(words1[2], tab[2])
        carry_pair(planes_tab, slice(0, S))

        for b in range(2):
            entries = list2[:, HALF * b // PER_COLUMN : HALF * (b + 1) // PER_COLUMN]
            nc.vector.tensor_copy(g_words2[:, HALF * b : HALF * (b + 1)], words2[:].bitcast(U32).indirect(entries))
        for b in range(2):
            nc.vector.tensor_copy(
                parted2[b][:].bitcast(U16).rearrange("p (h c n) -> p c h n", h=LP, n=GROUP),
                g_words2[:, HALF * b : HALF * (b + 1)].bitcast(U16).rearrange("p (c n h) -> p c h n", h=LP, n=GROUP),
            )

        nc.vector.quantize_mx(
            out=u_codes[:].bitcast(FP8X4),
            scales=u_scales[:],
            in_=u_bf[:].rearrange("p h n i -> p (h n i)"),
        )

        planes1 = [plane_first[:].bitcast(U8)] + [planes_tab[:].bitcast(U8)[:, S * s : S * (s + 1)] for s in range(KP - 1)]
        planes2 = [planes_tab2[:].bitcast(U8)[:, S * h : S * (h + 1)] for h in range(LP)]
        w_planes_u8 = w_planes[:].rearrange("p a n -> p (a n)").bitcast(U8)

        for b in range(2):
            for h in range(LP):
                for c in range(HALF // GROUP):
                    g = b * (HALF // GROUP) + c
                    first = 2 * (HALF * h + GROUP * c)
                    nc.tensor.matmul_mx(
                        out=banks[g][:, 0:GROUP],
                        lhsT=u_codes[:, M * h : M * (h + 1)].bitcast(FP8X4),
                        lhsT_scale=u_scales[:, M * h : M * (h + 1)],
                        rhs=parted2[b][:, first : first + 2 * GROUP].bitcast(FP4X4),
                        rhs_scale=planes2[h][:, GROUP * g : GROUP * (g + 1)],
                        start=(h == 0),
                        stop=False,
                    )

        def gather_and_multiply(a, pieces):
            done = 0
            for piece in pieces:
                entries = list1[:, done // PER_COLUMN : (done + piece) // PER_COLUMN]
                nc.vector.tensor_copy(g_words1[a][:, done : done + piece], words1[a][:].bitcast(U32).indirect(entries))
                for g in range(done // GROUP, (done + piece) // GROUP):
                    nc.tensor.matmul_mx(
                        out=banks[g][:, 0:GROUP],
                        lhsT=w_words[:, a, :].bitcast(FP4X4),
                        lhsT_scale=w_planes_u8[:, M * a : M * (a + 1)],
                        rhs=g_words1[a][:, GROUP * g : GROUP * (g + 1)].bitcast(FP8X4),
                        rhs_scale=planes1[a][:, GROUP * g : GROUP * (g + 1)],
                        start=False,
                        stop=(a == KP - 1),
                    )
                done += piece

        for a in range(KP - 1):
            gather_and_multiply(a, (S,))
        gather_and_multiply(KP - 1, (HALF, GROUP, GROUP))

        nc.scalar.copy(out_0[:, 0:GROUP], banks[0][:, 0:GROUP])
        nc.scalar.copy(out_0[:, GROUP:HALF], banks[1][:, 0:GROUP])
        nc.sync.dma_start(out[:, 0:HALF], out_0[:])
        nc.vector.tensor_copy(out_1[:, 0:GROUP], banks[2][:, 0:GROUP])
        nc.scalar.copy(out_1[:, GROUP:HALF], banks[3][:, 0:GROUP])
        nc.scalar.dma_start(out[:, HALF:S], out_1[:])
